import numpy as np, ml_dtypes
CORES = [17,81,89,18,82,90]
N = 6
DEG, TK = 3, 64
MASK = [[0,1,2],[0,1,2],[0,2,5],[0,3,4],[1,2,4],[0,2,5]]
def setup_inputs(rng):
    return {"x": rng.standard_normal((N, 128, TK), dtype=np.float32).astype(ml_dtypes.bfloat16), "w": rng.standard_normal((N, 128, DEG * 128), dtype=np.float32).astype(ml_dtypes.bfloat16)}
def setup_inputs_big(rng):
    d = setup_inputs(rng)
    for k in ("x", "w"): d[k] = (d[k].astype(np.float32) * 1024.0).astype(d[k].dtype)
    return d
def setup_inputs_small(rng):
    d = setup_inputs(rng)
    for k in ("x", "w"): d[k] = (d[k].astype(np.float32) * (1 / 1024.0)).astype(d[k].dtype)
    return d
def setup_inputs_apart(rng):
    d = setup_inputs(rng)
    f = (10.0 ** rng.permutation(np.linspace(-1.5, 1.5, N))).astype(np.float32).reshape(N, 1, 1)
    for k in ("x", "w"): d[k] = (d[k].astype(np.float32) * f).astype(d[k].dtype)
    return d
def reference(x, w):
    X, W = x.astype(np.float64), w.astype(np.float64)
    y = np.zeros((N, 128, TK))
    for r in range(N):
        for i, j in enumerate(MASK[r]):
            y[r] += W[r][:, 128 * i:128 * i + 128].T @ X[j]
    return {"y": y.astype(ml_dtypes.bfloat16 if x.dtype != np.float64 else np.float64)}

from concourse.bass import DstId, RemoteDMATransfer

N, DEG, TK, P = 6, 3, 64, 128
K_HOP = 2
K_FAN = 8
K_DIR = 4

SCRATCH = {
    "xd": ("dram", [P, TK], "bfloat16"),
    "rx": ("dram", [P, TK], "bfloat16"),
    "xs": ("sbuf", [P, TK], "bfloat16"),
    "ws": ("sbuf", [P, DEG * P], "bfloat16"),
    "ys": ("sbuf", [P, TK], "bfloat16"),
    "acc": ("psum", [P, TK], "float32"),
}
for _j in range(N):
    SCRATCH["in%d" % _j] = ("sbuf", [P, TK], "bfloat16")

SEMAPHORES = ["ldd", "ldx", "ldw", "sent", "rel", "mm", "cp", "st"] + ["s%d" % _j for _j in range(N)]


def _crossings(topo, a, b):
    ca, cb = topo.chip(a), topo.chip(b)
    if ca == cb:
        return 0
    return 1 if (topo.mates(ca, cb) or topo.same_plane(ca, cb)) else 2


def _plan(T, topo):
    cores, mask = list(T.cores), T.tables["MASK"]
    direct, relay, far = {}, {}, {}
    for j, src in enumerate(cores):
        dests = [cores[r] for r in range(len(cores)) if r != j and j in mask[r]]
        direct[j] = [d for d in dests if topo.may_write(src, d)]
        rest = [d for d in dests if not topo.may_write(src, d)]
        if rest:
            cand = [c for c in cores if c != src and c not in rest and topo.may_write(src, c)
                    and all(topo.may_write(c, d) for d in rest)]
            relay[j] = min(cand, key=lambda c: _crossings(topo, src, c) + sum(_crossings(topo, c, d) for d in rest))
            far[j] = rest
    return direct, relay, far


def _pick(bits, k):
    m = 0
    for b in bits[::len(bits) // k][:k]:
        m |= 1 << b
    return m


def rank_program(g, core, T, topo):
    rank = T.rank_of(core)
    if rank is None:
        return
    cores, sem = list(T.cores), T.sem
    direct, relay, far = _plan(T, topo)
    relays = list(relay.values())

    def width(c):
        return K_FAN if c in relays else K_DIR

    serves = [j for j in relay if relay[j] == core]
    assert len(serves) <= 1
    outs = list(direct[rank]) + ([relay[rank]] if rank in relay else []) + [d for j in serves for d in far[j]]

    if outs:
        g.sync.dma_start(T.xd[:, :], T.x[:, :]).then_inc(sem.ldd, 16)
    g.sync.dma_start(T.xs[:, :], T.x[:, :]).then_inc(sem.ldx, 16)
    g.sync.dma_start(T.ws[:, :], T.w[:, :]).then_inc(sem.ldw, 16)

    if outs:
        allowed = topo.mask(core, outs[0])
        for d in outs:
            allowed &= topo.mask(core, d)
        bits = [b for b in range(allowed.bit_length()) if (allowed >> b) & 1]
        k = width(core)

        def fan(src, j, dests):
            ids = []
            for d in dests:
                rid, pid, _se = topo.addr(d)
                ids.append(DstId(rid=rid, pnc=pid))
            g.remote_dma_fused([RemoteDMATransfer(dst_ids=ids, dma_engine_mask=_pick(bits, k),
                                                  remote_sem=sem["s%d" % j], srcs=[src[:, :]],
                                                  dsts=[T["in%d" % j][:, :] for _d in dests], alu_op=0)],
                               local_sem=sem.sent)
            return k

        left = 0
        g.wait_ge(sem.ldd, 16)
        if rank in relay:
            rid, pid, _se = topo.addr(relay[rank])
            g.remote_dma(out_ap=T.rx[:, :], in_ap=T.xd[:, :], remote_sem=sem.rel, local_sem=sem.sent,
                         pid=pid, routing_id=rid, dma_engine_mask=_pick(bits, K_HOP))
            left += K_HOP
        if direct[rank]:
            left += fan(T.xd, rank, direct[rank])
        for j in serves:
            g.wait_ge(sem.rel, K_HOP)
            left += fan(T.rx, j, far[j])
        g.wait_ge(sem.sent, left)

    terms = []
    for i, j in enumerate(T.tables["MASK"][rank]):
        if j == rank:
            terms.append(((0, 0), i, j, 0))
        elif core in direct[j]:
            terms.append(((1, _crossings(topo, cores[j], core)), i, j, width(cores[j])))
        else:
            terms.append(((2, _crossings(topo, relay[j], core)), i, j, width(relay[j])))
    terms.sort()
    g.tensor.wait_ge(sem.ldw, 16)
    for n, (_key, i, j, cnt) in enumerate(terms):
        if j == rank:
            g.tensor.wait_ge(sem.ldx, 16)
            rhs = T.xs
        else:
            g.tensor.wait_ge(sem["s%d" % j], cnt)
            rhs = T["in%d" % j]
        g.tensor.matmul(T.acc[:, :], T.ws[:, P * i:P * i + P], rhs[:, :],
                        start=(n == 0), stop=(n == len(terms) - 1)).then_inc(sem.mm, 1)

    g.vector.wait_ge(sem.mm, len(terms))
    g.vector.tensor_copy(T.ys[:, :], T.acc[:, :]).then_inc(sem.cp, 1)
    g.sync.wait_ge(sem.cp, 1)
    g.sync.dma_start(T.y[:, :], T.ys[:, :]).then_inc(sem.st, 16)
    g.sync.wait_ge(sem.st, 16)
